import numpy as np
import ml_dtypes


def mxq(x, axis, fmt="e4m3"):
    dtype, down = {"e4m3": (ml_dtypes.float8_e4m3fn, 7), "e5m2": (ml_dtypes.float8_e5m2, 14)}[fmt]
    v = np.moveaxis(np.asarray(x, np.float32).astype(ml_dtypes.bfloat16).astype(np.float64), axis, -1)
    blocks = v.reshape(v.shape[:-1] + (-1, 32))
    amax = np.abs(blocks).max(-1, keepdims=True)
    byte = np.maximum(np.where(amax > 0, np.frexp(amax)[1] - 1 + 127, 0) - down, 1)
    scale = np.exp2(byte - 127.0)
    codes = (blocks / scale).astype(np.float32).astype(dtype).astype(np.float64)
    return np.moveaxis((codes * scale).reshape(v.shape), -1, axis)


WIDE = False


def mx_kscale(k, group=512):
    if not WIDE:
        return np.ones(k)
    levels = np.array([18, -18])
    if group != 512:
        return np.exp2(np.random.permutation(np.resize(levels, k // group))).repeat(group)
    if k % 512:
        return np.exp2(np.random.permutation(np.resize(levels, k // 32))).repeat(32)
    a = np.empty((k // 512, 16))
    for p in range(k // 512):
        a[p, :8] = np.random.permutation(np.resize(levels, 8))
        for g in range(8):
            far = levels[np.abs(levels - a[p, g]) >= 10]
            a[p, g + 8] = far[np.random.randint(len(far))]
    return np.exp2(a.ravel()).repeat(32)


def f64(x):
    return np.asarray(x).astype(np.float64)


E2M1 = np.array([0.0, 0.5, 1.0, 1.5, 2.0, 3.0, 4.0, 6.0, -0.0, -0.5, -1.0, -1.5, -2.0, -3.0, -4.0, -6.0])


def pack_group(w):
    k, n = w.shape
    w = f64(np.asarray(w, np.float32).astype(ml_dtypes.bfloat16)).reshape(k // 32, 32, n)
    amax = np.abs(w).max(1)
    mant, ex = np.frexp(amax / 6.0)
    byte = np.clip(np.where(amax > 0, np.where(mant > 0.5, ex, ex - 1) + 127, 1), 1, 254)
    scaled = (w * np.exp2(127.0 - byte)[:, None, :]).reshape(k, n).astype(np.float32)
    c = np.ascontiguousarray(scaled.reshape(k // 4, 4, n).transpose(0, 2, 1)).astype(ml_dtypes.float4_e2m1fn).view(np.uint8) & 0xF
    return np.ascontiguousarray((c[..., 0::2] | (c[..., 1::2] << 4)).reshape(k // 4, 2 * n)), byte.astype(np.uint8)


def unpack_group(words, scales):
    p, n = words.shape[0], scales.shape[1]
    words = np.ascontiguousarray(words).reshape(p, n, 2)
    nib = np.empty((p, n, 4), np.uint8)
    nib[..., 0::2] = words & 0xF
    nib[..., 1::2] = words >> 4
    return E2M1[nib].transpose(0, 2, 1).reshape(4 * p, n) * np.repeat(np.exp2(scales.astype(np.float64) - 127.0), 32, axis=0)


G, D, M, N = 4, 128, 128, 1024


def setup_inputs():
    n = np.random.standard_normal
    s = mx_kscale(D, 0)[:, None]
    w_ = [pack_group(w) for w in n((G, D, M)) / np.sqrt(D) / s]
    return {
        "x": (n((G, D, N)) * s).astype(np.float32),
        "w_words": np.stack([w[0] for w in w_]),
        "w_scales": np.stack([w[1] for w in w_]),
        "b": (0.5 * n((G, M, 1))).astype(np.float32),
        "r": n((G, M, N)).astype(np.float32),
    }


def reference(x, w_words, w_scales, b, r):
    xq = mxq(f64(x), 1, "e4m3")
    y = np.stack([unpack_group(w_words[g], w_scales[g]) for g in range(G)]).transpose(0, 2, 1) @ xq
    y = y + f64(b)
    y = 1.0 / (1.0 + np.exp(-(y)))
    y = y + f64(r)
    return y

@@ -1,0 +1,100 @@
+from contextlib import ExitStack
+
+import concourse.mybir as mybir
+
+G, D, M, N = 4, 128, 128, 1024
+FLOPS = 2 * G * D * M * N
+
+F32 = mybir.dt.float32
+BF16 = mybir.dt.bfloat16
+I32 = mybir.dt.int32
+U32 = mybir.dt.uint32
+U8 = mybir.dt.uint8
+FP8X4 = mybir.dt.float8_e4m3fn_x4
+FP4X4 = mybir.dt.float4_e2m1fn_x4
+SIGMOID = mybir.ActivationFunctionType.Sigmoid
+
+P = 128
+PACK = 4
+ROWS = D // PACK
+HALF = 512
+SCALAR_COLS = 160
+
+
+def tile_rows_glin_sigmoid_bias_res_kernel(tc, x, w_words, w_scales, b, r, out):
+    nc = tc.nc
+    halves = [slice(h * HALF, (h + 1) * HALF) for h in range(N // HALF)]
+    pieces = [(h, g0) for h in range(N // HALF) for g0 in range(0, G, 2)]
+    x_rows = x.rearrange("g (p j) n -> (g p) j n", j=PACK)
+
+    with ExitStack() as ctx:
+        pool = ctx.enter_context(tc.tile_pool(name="sbuf", bufs=1))
+        psum = ctx.enter_context(tc.psum_pool(name="psum", bufs=1))
+        ctx.enter_context(tc.manual_schedule())
+
+        words = pool.tile([P, 2 * M], U8, align_bytes=64)
+        w_plane = pool.tile([P, M], U8, align_bytes=64)
+        b_rows = pool.tile([P, G, 32], F32, align_bytes=64)
+        bias = pool.tile([P, G, 32], F32, align_bytes=64)
+        warm = pool.tile([P, 8], F32)
+        raw = [pool.tile([P, PACK, HALF], F32, name="raw%d" % h) for h in range(2)]
+        grouped = [pool.tile([P, HALF, PACK], BF16, name="grouped%d" % h, align_bytes=64) for h in range(2)]
+        codes = [pool.tile([P, HALF], U32, name="codes%d" % h, align_bytes=64) for h in range(2)]
+        x_plane = [pool.tile([P, HALF], U8, name="x_plane%d" % h, align_bytes=64) for h in range(2)]
+        res = [pool.tile([P, 2, HALF], F32, name="res%d" % i) for i in range(len(pieces))]
+        y = [pool.tile([P, 2, HALF], F32, name="y%d" % i) for i in range(len(pieces))]
+        acc = {(h, g): psum.tile([M, HALF], F32, name="acc%d_%d" % (h, g)) for h in range(2) for g in range(G)}
+
+        nc.vector.memset(w_plane[:].bitcast(I32), 0)
+        nc.vector.memset(b_rows[:], 0.0)
+        nc.scalar.activation(out=warm[:, 0:1], in_=b_rows[:, 0, 0:1], func=SIGMOID)
+
+        nc.sync.dma_start(out=raw[0][:], in_=x_rows[:, :, halves[0]])
+        nc.sync.dma_start(out=words[:], in_=w_words.rearrange("g p c -> (g p) c"))
+        for g in range(G):
+            nc.sync.dma_start(out=w_plane[ROWS * g : ROWS * g + 4, :].bitcast(I32), in_=w_scales[g].bitcast(I32))
+        nc.sync.dma_start(out=b_rows[0:P:32, :, :], in_=b.rearrange("g (q j) o -> q g (j o)", j=32))
+        nc.sync.dma_start(out=raw[1][:], in_=x_rows[:, :, halves[1]])
+        for i, (h, g0) in enumerate(pieces):
+            nc.sync.dma_start(out=res[i][:], in_=r[g0 : g0 + 2, :, halves[h]].rearrange("g m n -> m g n"))
+
+        def interleave(h):
+            for copy, cols in (
+                (nc.scalar.copy, slice(0, SCALAR_COLS)),
+                (nc.vector.tensor_copy, slice(SCALAR_COLS, HALF)),
+            ):
+                copy(
+                    out=grouped[h][:, cols, :].rearrange("p (c i) t -> p c t i", i=4),
+                    in_=raw[h][:, :, cols].rearrange("p t (c i) -> p c t i", i=4),
+                )
+
+        def quantize_and_multiply(h):
+            nc.vector.quantize_mx(
+                out=codes[h][:].bitcast(FP8X4),
+                scales=x_plane[h][:],
+                in_=grouped[h][:].rearrange("p c t -> p (c t)"),
+            )
+            for g in range(G):
+                rows = slice(ROWS * g, ROWS * (g + 1))
+                nc.tensor.matmul_mx(
+                    out=acc[h, g][:],
+                    lhsT=words[rows, :].bitcast(FP4X4),
+                    lhsT_scale=w_plane[rows, :],
+                    rhs=codes[h][rows, :].bitcast(FP8X4),
+                    rhs_scale=x_plane[h][rows, :],
+                    start=True,
+                    stop=True,
+                )
+
+        interleave(0)
+        nc.vector.transpose(out=bias[:].rearrange("p g j -> p (g j)"), in_=b_rows[:].rearrange("p g j -> p (g j)"))
+        quantize_and_multiply(0)
+        interleave(1)
+        quantize_and_multiply(1)
+
+        for i, (h, g0) in enumerate(pieces):
+            for k in range(2):
+                g = g0 + k
+                nc.scalar.activation(out=y[i][:, k, :], in_=acc[h, g][:], func=SIGMOID, bias=bias[:, g, 0:1])
+                nc.vector.tensor_add(out=y[i][:, k, :], in0=y[i][:, k, :], in1=res[i][:, k, :])
+            nc.sync.dma_start(out=out[g0 : g0 + 2, :, halves[h]].rearrange("g m n -> m g n"), in_=y[i][:])

@@ -37,12 +37,12 @@ def tile_rows_glin_sigmoid_bias_res_kernel(tc, x, w_words, w_scales, b, r, out):
         b_rows = pool.tile([P, G, 32], F32, align_bytes=64)
         bias = pool.tile([P, G, 32], F32, align_bytes=64)
         warm = pool.tile([P, 8], F32)
-        raw = [pool.tile([P, PACK, HALF], F32, name="raw%d" % h) for h in range(2)]
+        raw = [pool.tile([P, PACK, HALF], F32, name="raw%d" % h, align_bytes=256) for h in range(2)]
         grouped = [pool.tile([P, HALF, PACK], BF16, name="grouped%d" % h, align_bytes=64) for h in range(2)]
         codes = [pool.tile([P, HALF], U32, name="codes%d" % h, align_bytes=64) for h in range(2)]
         x_plane = [pool.tile([P, HALF], U8, name="x_plane%d" % h, align_bytes=64) for h in range(2)]
-        res = [pool.tile([P, 2, HALF], F32, name="res%d" % i) for i in range(len(pieces))]
-        y = [pool.tile([P, 2, HALF], F32, name="y%d" % i) for i in range(len(pieces))]
+        res = [pool.tile([P, 2, HALF], F32, name="res%d" % i, align_bytes=256) for i in range(len(pieces))]
+        y = [pool.tile([P, 2, HALF], F32, name="y%d" % i, align_bytes=256) for i in range(len(pieces))]
         acc = {(h, g): psum.tile([M, HALF], F32, name="acc%d_%d" % (h, g)) for h in range(2) for g in range(G)}
 
         nc.vector.memset(w_plane[:].bitcast(I32), 0)

@@ -18,7 +18,11 @@ P = 128
 PACK = 4
 ROWS = D // PACK
 HALF = 512
-SCALAR_COLS = 160
+QUARTER = HALF // 2
+FIRST = HALF + 128
+SCALAR_FIRST = 160
+SCALAR_SECOND = 96
+DMA_ALIGN = 256
 
 
 def tile_rows_glin_sigmoid_bias_res_kernel(tc, x, w_words, w_scales, b, r, out):
@@ -32,65 +36,78 @@ def tile_rows_glin_sigmoid_bias_res_kernel(tc, x, w_words, w_scales, b, r, out):
         psum = ctx.enter_context(tc.psum_pool(name="psum", bufs=1))
         ctx.enter_context(tc.manual_schedule())
 
-        words = pool.tile([P, 2 * M], U8, align_bytes=64)
+        words = pool.tile([P, 2 * M], U8, align_bytes=DMA_ALIGN)
         w_plane = pool.tile([P, M], U8, align_bytes=64)
         b_rows = pool.tile([P, G, 32], F32, align_bytes=64)
         bias = pool.tile([P, G, 32], F32, align_bytes=64)
         warm = pool.tile([P, 8], F32)
-        raw = [pool.tile([P, PACK, HALF], F32, name="raw%d" % h, align_bytes=256) for h in range(2)]
-        grouped = [pool.tile([P, HALF, PACK], BF16, name="grouped%d" % h, align_bytes=64) for h in range(2)]
-        codes = [pool.tile([P, HALF], U32, name="codes%d" % h, align_bytes=64) for h in range(2)]
-        x_plane = [pool.tile([P, HALF], U8, name="x_plane%d" % h, align_bytes=64) for h in range(2)]
-        res = [pool.tile([P, 2, HALF], F32, name="res%d" % i, align_bytes=256) for i in range(len(pieces))]
-        y = [pool.tile([P, 2, HALF], F32, name="y%d" % i, align_bytes=256) for i in range(len(pieces))]
+        raw_first = pool.tile([P, PACK, FIRST], F32, align_bytes=DMA_ALIGN)
+        raw_second = pool.tile([P, PACK, N - FIRST], F32, align_bytes=DMA_ALIGN)
+        grouped = pool.tile([P, N, PACK], BF16, align_bytes=64)
+        codes = pool.tile([P, N], U32, align_bytes=64)
+        x_plane = pool.tile([P, N], U8, align_bytes=64)
+        res = [pool.tile([P, 2, HALF], F32, name="res%d" % i, align_bytes=DMA_ALIGN) for i in range(len(pieces))]
+        y = [pool.tile([P, 2, HALF], F32, name="y%d" % i, align_bytes=DMA_ALIGN) for i in range(len(pieces))]
         acc = {(h, g): psum.tile([M, HALF], F32, name="acc%d_%d" % (h, g)) for h in range(2) for g in range(G)}
 
-        nc.vector.memset(w_plane[:].bitcast(I32), 0)
         nc.vector.memset(b_rows[:], 0.0)
-        nc.scalar.activation(out=warm[:, 0:1], in_=b_rows[:, 0, 0:1], func=SIGMOID)
+        nc.vector.memset(warm[:], 0.0)
+        nc.vector.memset(w_plane[:].bitcast(I32), 0)
 
-        nc.sync.dma_start(out=raw[0][:], in_=x_rows[:, :, halves[0]])
+        nc.sync.dma_start(out=raw_first[:], in_=x_rows[:, :, 0:FIRST])
         nc.sync.dma_start(out=words[:], in_=w_words.rearrange("g p c -> (g p) c"))
+        nc.sync.dma_start(out=b_rows[0:P:32, :, :], in_=b.rearrange("g (q j) o -> q g (j o)", j=32))
         for g in range(G):
             nc.sync.dma_start(out=w_plane[ROWS * g : ROWS * g + 4, :].bitcast(I32), in_=w_scales[g].bitcast(I32))
-        nc.sync.dma_start(out=b_rows[0:P:32, :, :], in_=b.rearrange("g (q j) o -> q g (j o)", j=32))
-        nc.sync.dma_start(out=raw[1][:], in_=x_rows[:, :, halves[1]])
+        nc.sync.dma_start(out=raw_second[:], in_=x_rows[:, :, FIRST:N])
         for i, (h, g0) in enumerate(pieces):
             nc.sync.dma_start(out=res[i][:], in_=r[g0 : g0 + 2, :, halves[h]].rearrange("g m n -> m g n"))
 
-        def interleave(h):
-            for copy, cols in (
-                (nc.scalar.copy, slice(0, SCALAR_COLS)),
-                (nc.vector.tensor_copy, slice(SCALAR_COLS, HALF)),
-            ):
-                copy(
-                    out=grouped[h][:, cols, :].rearrange("p (c i) t -> p c t i", i=4),
-                    in_=raw[h][:, :, cols].rearrange("p t (c i) -> p c t i", i=4),
-                )
+        nc.scalar.activation(out=warm[:, 0:1], in_=warm[:, 0:1], func=SIGMOID)
 
-        def quantize_and_multiply(h):
-            nc.vector.quantize_mx(
-                out=codes[h][:].bitcast(FP8X4),
-                scales=x_plane[h][:],
-                in_=grouped[h][:].rearrange("p c t -> p (c t)"),
+        def interleave(copy, c0, c1):
+            raw, base = (raw_first, 0) if c0 < FIRST else (raw_second, FIRST)
+            copy(
+                out=grouped[:, c0:c1, :].rearrange("p (c i) t -> p c t i", i=4),
+                in_=raw[:, :, c0 - base : c1 - base].rearrange("p t (c i) -> p c t i", i=4),
             )
+
+        def quantize(c0, c1):
+            nc.vector.quantize_mx(
+                out=codes[:, c0:c1].bitcast(FP8X4),
+                scales=x_plane[:, c0:c1],
+                in_=grouped[:, c0:c1, :].rearrange("p c t -> p (c t)"),
+            )
+
+        def multiply(h):
             for g in range(G):
                 rows = slice(ROWS * g, ROWS * (g + 1))
                 nc.tensor.matmul_mx(
                     out=acc[h, g][:],
                     lhsT=words[rows, :].bitcast(FP4X4),
                     lhsT_scale=w_plane[rows, :],
-                    rhs=codes[h][rows, :].bitcast(FP8X4),
-                    rhs_scale=x_plane[h][rows, :],
+                    rhs=codes[rows, halves[h]].bitcast(FP8X4),
+                    rhs_scale=x_plane[rows, halves[h]],
                     start=True,
                     stop=True,
                 )
 
-        interleave(0)
+        interleave(nc.scalar.copy, 0, SCALAR_FIRST)
+        interleave(nc.vector.tensor_copy, QUARTER, HALF)
+        interleave(nc.vector.tensor_copy, SCALAR_FIRST, QUARTER)
+        quantize(QUARTER, HALF)
+        quantize(0, QUARTER)
+        multiply(0)
         nc.vector.transpose(out=bias[:].rearrange("p g j -> p (g j)"), in_=b_rows[:].rearrange("p g j -> p (g j)"))
-        quantize_and_multiply(0)
-        interleave(1)
-        quantize_and_multiply(1)
+        interleave(nc.scalar.copy, HALF, FIRST)
+        quantize(HALF, FIRST)
+
+        interleave(nc.scalar.copy, FIRST, FIRST + SCALAR_SECOND)
+        interleave(nc.vector.tensor_copy, N - QUARTER, N)
+        interleave(nc.vector.tensor_copy, FIRST + SCALAR_SECOND, N - QUARTER)
+        quantize(N - QUARTER, N)
+        quantize(FIRST, N - QUARTER)
+        multiply(1)
 
         for i, (h, g0) in enumerate(pieces):
             for k in range(2):

@@ -19,9 +19,7 @@ PACK = 4
 ROWS = D // PACK
 HALF = 512
 QUARTER = HALF // 2
-FIRST = HALF + 128
-SCALAR_FIRST = 160
-SCALAR_SECOND = 96
+FIRST = HALF
 DMA_ALIGN = 256
 
 
@@ -40,7 +38,6 @@ def tile_rows_glin_sigmoid_bias_res_kernel(tc, x, w_words, w_scales, b, r, out):
         w_plane = pool.tile([P, M], U8, align_bytes=64)
         b_rows = pool.tile([P, G, 32], F32, align_bytes=64)
         bias = pool.tile([P, G, 32], F32, align_bytes=64)
-        warm = pool.tile([P, 8], F32)
         raw_first = pool.tile([P, PACK, FIRST], F32, align_bytes=DMA_ALIGN)
         raw_second = pool.tile([P, PACK, N - FIRST], F32, align_bytes=DMA_ALIGN)
         grouped = pool.tile([P, N, PACK], BF16, align_bytes=64)
@@ -51,7 +48,6 @@ def tile_rows_glin_sigmoid_bias_res_kernel(tc, x, w_words, w_scales, b, r, out):
         acc = {(h, g): psum.tile([M, HALF], F32, name="acc%d_%d" % (h, g)) for h in range(2) for g in range(G)}
 
         nc.vector.memset(b_rows[:], 0.0)
-        nc.vector.memset(warm[:], 0.0)
         nc.vector.memset(w_plane[:].bitcast(I32), 0)
 
         nc.sync.dma_start(out=raw_first[:], in_=x_rows[:, :, 0:FIRST])
@@ -63,11 +59,10 @@ def tile_rows_glin_sigmoid_bias_res_kernel(tc, x, w_words, w_scales, b, r, out):
         for i, (h, g0) in enumerate(pieces):
             nc.sync.dma_start(out=res[i][:], in_=r[g0 : g0 + 2, :, halves[h]].rearrange("g m n -> m g n"))
 
-        nc.scalar.activation(out=warm[:, 0:1], in_=warm[:, 0:1], func=SIGMOID)
 
-        def interleave(copy, c0, c1):
+        def interleave(c0, c1):
             raw, base = (raw_first, 0) if c0 < FIRST else (raw_second, FIRST)
-            copy(
+            nc.vector.tensor_copy(
                 out=grouped[:, c0:c1, :].rearrange("p (c i) t -> p c t i", i=4),
                 in_=raw[:, :, c0 - base : c1 - base].rearrange("p t (c i) -> p c t i", i=4),
             )
@@ -92,22 +87,16 @@ def tile_rows_glin_sigmoid_bias_res_kernel(tc, x, w_words, w_scales, b, r, out):
                     stop=True,
                 )
 
-        interleave(nc.scalar.copy, 0, SCALAR_FIRST)
-        interleave(nc.vector.tensor_copy, QUARTER, HALF)
-        interleave(nc.vector.tensor_copy, SCALAR_FIRST, QUARTER)
-        quantize(QUARTER, HALF)
-        quantize(0, QUARTER)
-        multiply(0)
-        nc.vector.transpose(out=bias[:].rearrange("p g j -> p (g j)"), in_=b_rows[:].rearrange("p g j -> p (g j)"))
-        interleave(nc.scalar.copy, HALF, FIRST)
-        quantize(HALF, FIRST)
-
-        interleave(nc.scalar.copy, FIRST, FIRST + SCALAR_SECOND)
-        interleave(nc.vector.tensor_copy, N - QUARTER, N)
-        interleave(nc.vector.tensor_copy, FIRST + SCALAR_SECOND, N - QUARTER)
-        quantize(N - QUARTER, N)
-        quantize(FIRST, N - QUARTER)
-        multiply(1)
+        for h in range(2):
+            if h == 0:
+                interleave(0, HALF)
+                nc.vector.transpose(out=bias[:].rearrange("p g j -> p (g j)"), in_=b_rows[:].rearrange("p g j -> p (g j)"))
+                quantize(0, HALF)
+            else:
+                for step in (interleave, quantize):
+                    for c0 in range(HALF, N, QUARTER):
+                        step(c0, c0 + QUARTER)
+            multiply(h)
 
         for i, (h, g0) in enumerate(pieces):
             for k in range(2):

@@ -19,88 +19,109 @@ PACK = 4
 ROWS = D // PACK
 HALF = 512
 QUARTER = HALF // 2
-FIRST = HALF
-DMA_ALIGN = 256
+VECTOR_COLS = 320
+DMA_ALIGN = 4096
+PERIOD = 14
+REPEATS = 5
 
 
 def tile_rows_glin_sigmoid_bias_res_kernel(tc, x, w_words, w_scales, b, r, out):
     nc = tc.nc
     halves = [slice(h * HALF, (h + 1) * HALF) for h in range(N // HALF)]
-    pieces = [(h, g0) for h in range(N // HALF) for g0 in range(0, G, 2)]
+    r_blocks = [(0, 2, 0, 1), (2, 4, 0, 1), (0, 2, 1, 2), (2, 4, 1, 2)]
+    out_blocks = [(0, 2, 0, 1), (2, 4, 0, 1), (0, 2, 1, 2), (2, 4, 1, 2)]
     x_rows = x.rearrange("g (p j) n -> (g p) j n", j=PACK)
+
+    def units(block):
+        g0, g1, h0, h1 = block
+        return [(h, g) for g in range(g0, g1) for h in range(h0, h1)]
+
+    def in_hbm(t, block):
+        g0, g1, h0, h1 = block
+        return t[g0:g1, :, h0 * HALF : h1 * HALF].rearrange("g m n -> m g n")
 
     with ExitStack() as ctx:
         pool = ctx.enter_context(tc.tile_pool(name="sbuf", bufs=1))
         psum = ctx.enter_context(tc.psum_pool(name="psum", bufs=1))
         ctx.enter_context(tc.manual_schedule())
 
-        words = pool.tile([P, 2 * M], U8, align_bytes=DMA_ALIGN)
+        def block_tiles(name, blocks):
+            tiles, views = [], {}
+            for i, (g0, g1, h0, h1) in enumerate(blocks):
+                t = pool.tile([P, g1 - g0, (h1 - h0) * HALF], F32, name="%s%d" % (name, i), align_bytes=DMA_ALIGN)
+                tiles.append(t)
+                for h, g in units((g0, g1, h0, h1)):
+                    views[h, g] = t[:, g - g0, (h - h0) * HALF : (h - h0 + 1) * HALF]
+            return tiles, views
+
+        words = pool.tile([P, 2 * M], U8, align_bytes=256)
         w_plane = pool.tile([P, M], U8, align_bytes=64)
         b_rows = pool.tile([P, G, 32], F32, align_bytes=64)
         bias = pool.tile([P, G, 32], F32, align_bytes=64)
-        raw_first = pool.tile([P, PACK, FIRST], F32, align_bytes=DMA_ALIGN)
-        raw_second = pool.tile([P, PACK, N - FIRST], F32, align_bytes=DMA_ALIGN)
+        warm = pool.tile([P, 1], F32)
+        raw = [pool.tile([P, PACK, HALF], F32, name="raw%d" % h, align_bytes=DMA_ALIGN) for h in range(2)]
         grouped = pool.tile([P, N, PACK], BF16, align_bytes=64)
         codes = pool.tile([P, N], U32, align_bytes=64)
         x_plane = pool.tile([P, N], U8, align_bytes=64)
-        res = [pool.tile([P, 2, HALF], F32, name="res%d" % i, align_bytes=DMA_ALIGN) for i in range(len(pieces))]
-        y = [pool.tile([P, 2, HALF], F32, name="y%d" % i, align_bytes=DMA_ALIGN) for i in range(len(pieces))]
+        r_tiles, res = block_tiles("res", r_blocks)
+        y_tiles, y = block_tiles("y", out_blocks)
         acc = {(h, g): psum.tile([M, HALF], F32, name="acc%d_%d" % (h, g)) for h in range(2) for g in range(G)}
 
         nc.vector.memset(b_rows[:], 0.0)
         nc.vector.memset(w_plane[:].bitcast(I32), 0)
+        nc.vector.memset(warm[:], 0.0)
+        nc.scalar.activation(out=warm[:], in_=warm[:], func=SIGMOID)
 
-        nc.sync.dma_start(out=raw_first[:], in_=x_rows[:, :, 0:FIRST])
+        nc.sync.dma_start(out=raw[0][:], in_=x_rows[:, :, halves[0]])
         nc.sync.dma_start(out=words[:], in_=w_words.rearrange("g p c -> (g p) c"))
         nc.sync.dma_start(out=b_rows[0:P:32, :, :], in_=b.rearrange("g (q j) o -> q g (j o)", j=32))
         for g in range(G):
             nc.sync.dma_start(out=w_plane[ROWS * g : ROWS * g + 4, :].bitcast(I32), in_=w_scales[g].bitcast(I32))
-        nc.sync.dma_start(out=raw_second[:], in_=x_rows[:, :, FIRST:N])
-        for i, (h, g0) in enumerate(pieces):
-            nc.sync.dma_start(out=res[i][:], in_=r[g0 : g0 + 2, :, halves[h]].rearrange("g m n -> m g n"))
+        nc.sync.dma_start(out=raw[1][:], in_=x_rows[:, :, halves[1]])
+        for i, block in enumerate(r_blocks):
+            nc.sync.dma_start(out=r_tiles[i][:], in_=in_hbm(r, block))
 
-
-        def interleave(c0, c1):
-            raw, base = (raw_first, 0) if c0 < FIRST else (raw_second, FIRST)
-            nc.vector.tensor_copy(
-                out=grouped[:, c0:c1, :].rearrange("p (c i) t -> p c t i", i=4),
-                in_=raw[:, :, c0 - base : c1 - base].rearrange("p t (c i) -> p c t i", i=4),
+        def interleave(copy, h, c0, c1):
+            copy(
+                out=grouped[:, h * HALF + c0 : h * HALF + c1, :].rearrange("p (c i) t -> p c t i", i=4),
+                in_=raw[h][:, :, c0:c1].rearrange("p t (c i) -> p c t i", i=4),
             )
 
-        def quantize(c0, c1):
+        def quantize(h, c0, c1):
+            cols = slice(h * HALF + c0, h * HALF + c1)
             nc.vector.quantize_mx(
-                out=codes[:, c0:c1].bitcast(FP8X4),
-                scales=x_plane[:, c0:c1],
-                in_=grouped[:, c0:c1, :].rearrange("p c t -> p (c t)"),
+                out=codes[:, cols].bitcast(FP8X4),
+                scales=x_plane[:, cols],
+                in_=grouped[:, cols, :].rearrange("p c t -> p (c t)"),
             )
 
-        def multiply(h):
-            for g in range(G):
-                rows = slice(ROWS * g, ROWS * (g + 1))
-                nc.tensor.matmul_mx(
-                    out=acc[h, g][:],
-                    lhsT=words[rows, :].bitcast(FP4X4),
-                    lhsT_scale=w_plane[rows, :],
-                    rhs=codes[rows, halves[h]].bitcast(FP8X4),
-                    rhs_scale=x_plane[rows, halves[h]],
-                    start=True,
-                    stop=True,
-                )
+        def multiply(h, g):
+            rows = slice(ROWS * g, ROWS * (g + 1))
+            nc.tensor.matmul_mx(
+                out=acc[h, g][:],
+                lhsT=words[rows, :].bitcast(FP4X4),
+                lhsT_scale=w_plane[rows, :],
+                rhs=codes[rows, halves[h]].bitcast(FP8X4),
+                rhs_scale=x_plane[rows, halves[h]],
+                start=True,
+                stop=True,
+            )
 
+        order = [u for block in out_blocks for u in units(block)]
         for h in range(2):
+            interleave(nc.scalar.copy, h, VECTOR_COLS, HALF)
+            interleave(nc.vector.tensor_copy, h, 0, QUARTER)
+            interleave(nc.vector.tensor_copy, h, QUARTER, VECTOR_COLS)
+            quantize(h, 0, QUARTER)
+            quantize(h, QUARTER, HALF)
             if h == 0:
-                interleave(0, HALF)
                 nc.vector.transpose(out=bias[:].rearrange("p g j -> p (g j)"), in_=b_rows[:].rearrange("p g j -> p (g j)"))
-                quantize(0, HALF)
-            else:
-                for step in (interleave, quantize):
-                    for c0 in range(HALF, N, QUARTER):
-                        step(c0, c0 + QUARTER)
-            multiply(h)
+            for hh, g in order:
+                if hh == h:
+                    multiply(h, g)
 
-        for i, (h, g0) in enumerate(pieces):
-            for k in range(2):
-                g = g0 + k
-                nc.scalar.activation(out=y[i][:, k, :], in_=acc[h, g][:], func=SIGMOID, bias=bias[:, g, 0:1])
-                nc.vector.tensor_add(out=y[i][:, k, :], in0=y[i][:, k, :], in1=res[i][:, k, :])
-            nc.sync.dma_start(out=out[g0 : g0 + 2, :, halves[h]].rearrange("g m n -> m g n"), in_=y[i][:])
+        for i, block in enumerate(out_blocks):
+            for h, g in units(block):
+                nc.scalar.activation(out=y[h, g], in_=acc[h, g][:], func=SIGMOID, bias=bias[:, g, 0:1])
+                nc.vector.tensor_add(out=y[h, g], in0=y[h, g], in1=res[h, g])
+            nc.sync.dma_start(out=in_hbm(out, block), in_=y_tiles[i][:])

@@ -19,10 +19,10 @@ PACK = 4
 ROWS = D // PACK
 HALF = 512
 QUARTER = HALF // 2
-VECTOR_COLS = 320
-DMA_ALIGN = 4096
-PERIOD = 14
-REPEATS = 5
+FIRST = 576
+SCALAR_LAST = 128
+VECTOR_COLS = 336
+DMA_ALIGN = 256
 
 
 def tile_rows_glin_sigmoid_bias_res_kernel(tc, x, w_words, w_scales, b, r, out):
@@ -59,7 +59,7 @@ def tile_rows_glin_sigmoid_bias_res_kernel(tc, x, w_words, w_scales, b, r, out):
         b_rows = pool.tile([P, G, 32], F32, align_bytes=64)
         bias = pool.tile([P, G, 32], F32, align_bytes=64)
         warm = pool.tile([P, 1], F32)
-        raw = [pool.tile([P, PACK, HALF], F32, name="raw%d" % h, align_bytes=DMA_ALIGN) for h in range(2)]
+        raw = [pool.tile([P, PACK, w], F32, name="raw%d" % i, align_bytes=DMA_ALIGN) for i, w in enumerate((FIRST, N - FIRST))]
         grouped = pool.tile([P, N, PACK], BF16, align_bytes=64)
         codes = pool.tile([P, N], U32, align_bytes=64)
         x_plane = pool.tile([P, N], U8, align_bytes=64)
@@ -72,27 +72,27 @@ def tile_rows_glin_sigmoid_bias_res_kernel(tc, x, w_words, w_scales, b, r, out):
         nc.vector.memset(warm[:], 0.0)
         nc.scalar.activation(out=warm[:], in_=warm[:], func=SIGMOID)
 
-        nc.sync.dma_start(out=raw[0][:], in_=x_rows[:, :, halves[0]])
+        nc.sync.dma_start(out=raw[0][:], in_=x_rows[:, :, 0:FIRST])
         nc.sync.dma_start(out=words[:], in_=w_words.rearrange("g p c -> (g p) c"))
         nc.sync.dma_start(out=b_rows[0:P:32, :, :], in_=b.rearrange("g (q j) o -> q g (j o)", j=32))
         for g in range(G):
             nc.sync.dma_start(out=w_plane[ROWS * g : ROWS * g + 4, :].bitcast(I32), in_=w_scales[g].bitcast(I32))
-        nc.sync.dma_start(out=raw[1][:], in_=x_rows[:, :, halves[1]])
+        nc.sync.dma_start(out=raw[1][:], in_=x_rows[:, :, FIRST:N])
         for i, block in enumerate(r_blocks):
             nc.sync.dma_start(out=r_tiles[i][:], in_=in_hbm(r, block))
 
-        def interleave(copy, h, c0, c1):
+        def interleave(copy, c0, c1):
+            src, base = (raw[0], 0) if c0 < FIRST else (raw[1], FIRST)
             copy(
-                out=grouped[:, h * HALF + c0 : h * HALF + c1, :].rearrange("p (c i) t -> p c t i", i=4),
-                in_=raw[h][:, :, c0:c1].rearrange("p t (c i) -> p c t i", i=4),
+                out=grouped[:, c0:c1, :].rearrange("p (c i) t -> p c t i", i=4),
+                in_=src[:, :, c0 - base : c1 - base].rearrange("p t (c i) -> p c t i", i=4),
             )
 
-        def quantize(h, c0, c1):
-            cols = slice(h * HALF + c0, h * HALF + c1)
+        def quantize(c0, c1):
             nc.vector.quantize_mx(
-                out=codes[:, cols].bitcast(FP8X4),
-                scales=x_plane[:, cols],
-                in_=grouped[:, cols, :].rearrange("p c t -> p (c t)"),
+                out=codes[:, c0:c1].bitcast(FP8X4),
+                scales=x_plane[:, c0:c1],
+                in_=grouped[:, c0:c1, :].rearrange("p c t -> p (c t)"),
             )
 
         def multiply(h, g):
@@ -108,17 +108,24 @@ def tile_rows_glin_sigmoid_bias_res_kernel(tc, x, w_words, w_scales, b, r, out):
             )
 
         order = [u for block in out_blocks for u in units(block)]
-        for h in range(2):
-            interleave(nc.scalar.copy, h, VECTOR_COLS, HALF)
-            interleave(nc.vector.tensor_copy, h, 0, QUARTER)
-            interleave(nc.vector.tensor_copy, h, QUARTER, VECTOR_COLS)
-            quantize(h, 0, QUARTER)
-            quantize(h, QUARTER, HALF)
+        interleave(nc.scalar.copy, VECTOR_COLS, HALF)
+        interleave(nc.scalar.copy, HALF, FIRST)
+        interleave(nc.vector.tensor_copy, 0, QUARTER)
+        interleave(nc.vector.tensor_copy, QUARTER, VECTOR_COLS)
+        quantize(0, QUARTER)
+        quantize(QUARTER, HALF)
+        nc.vector.transpose(out=bias[:].rearrange("p g j -> p (g j)"), in_=b_rows[:].rearrange("p g j -> p (g j)"))
+        for h, g in order:
             if h == 0:
-                nc.vector.transpose(out=bias[:].rearrange("p g j -> p (g j)"), in_=b_rows[:].rearrange("p g j -> p (g j)"))
-            for hh, g in order:
-                if hh == h:
-                    multiply(h, g)
+                multiply(h, g)
+        interleave(nc.scalar.copy, N - SCALAR_LAST, N)
+        interleave(nc.vector.tensor_copy, FIRST, HALF + QUARTER)
+        interleave(nc.vector.tensor_copy, HALF + QUARTER, N - SCALAR_LAST)
+        quantize(HALF, HALF + QUARTER)
+        quantize(HALF + QUARTER, N)
+        for h, g in order:
+            if h == 1:
+                multiply(h, g)
 
         for i, block in enumerate(out_blocks):
             for h, g in units(block):

@@ -72,12 +72,16 @@ def tile_rows_glin_sigmoid_bias_res_kernel(tc, x, w_words, w_scales, b, r, out):
         nc.vector.memset(warm[:], 0.0)
         nc.scalar.activation(out=warm[:], in_=warm[:], func=SIGMOID)
 
+        def load_scales(g):
+            nc.sync.dma_start(out=w_plane[ROWS * g : ROWS * g + 4, :].bitcast(I32), in_=w_scales[g].bitcast(I32))
+
         nc.sync.dma_start(out=raw[0][:], in_=x_rows[:, :, 0:FIRST])
         nc.sync.dma_start(out=words[:], in_=w_words.rearrange("g p c -> (g p) c"))
         nc.sync.dma_start(out=b_rows[0:P:32, :, :], in_=b.rearrange("g (q j) o -> q g (j o)", j=32))
-        for g in range(G):
-            nc.sync.dma_start(out=w_plane[ROWS * g : ROWS * g + 4, :].bitcast(I32), in_=w_scales[g].bitcast(I32))
+        load_scales(0)
         nc.sync.dma_start(out=raw[1][:], in_=x_rows[:, :, FIRST:N])
+        for g in range(1, G):
+            load_scales(g)
         for i, block in enumerate(r_blocks):
             nc.sync.dma_start(out=r_tiles[i][:], in_=in_hbm(r, block))
 

@@ -70,18 +70,17 @@ def tile_rows_glin_sigmoid_bias_res_kernel(tc, x, w_words, w_scales, b, r, out):
         nc.vector.memset(b_rows[:], 0.0)
         nc.vector.memset(w_plane[:].bitcast(I32), 0)
         nc.vector.memset(warm[:], 0.0)
-        nc.scalar.activation(out=warm[:], in_=warm[:], func=SIGMOID)
 
         def load_scales(g):
-            nc.sync.dma_start(out=w_plane[ROWS * g : ROWS * g + 4, :].bitcast(I32), in_=w_scales[g].bitcast(I32))
+            nc.scalar.dma_start(out=w_plane[ROWS * g : ROWS * g + 4, :].bitcast(I32), in_=w_scales[g].bitcast(I32))
 
+        nc.scalar.dma_start(out=words[:].bitcast(I32), in_=w_words.rearrange("g p c -> (g p) c").bitcast(I32))
         nc.sync.dma_start(out=raw[0][:], in_=x_rows[:, :, 0:FIRST])
-        nc.sync.dma_start(out=words[:], in_=w_words.rearrange("g p c -> (g p) c"))
-        nc.sync.dma_start(out=b_rows[0:P:32, :, :], in_=b.rearrange("g (q j) o -> q g (j o)", j=32))
-        load_scales(0)
-        nc.sync.dma_start(out=raw[1][:], in_=x_rows[:, :, FIRST:N])
-        for g in range(1, G):
+        nc.scalar.dma_start(out=b_rows[0:P:32, :, :], in_=b.rearrange("g (q j) o -> q g (j o)", j=32))
+        for g in range(G):
             load_scales(g)
+        nc.scalar.activation(out=warm[:], in_=warm[:], func=SIGMOID)
+        nc.sync.dma_start(out=raw[1][:], in_=x_rows[:, :, FIRST:N])
         for i, block in enumerate(r_blocks):
             nc.sync.dma_start(out=r_tiles[i][:], in_=in_hbm(r, block))
 

@@ -20,7 +20,7 @@ ROWS = D // PACK
 HALF = 512
 QUARTER = HALF // 2
 FIRST = 576
-SCALAR_LAST = 128
+SCALAR_LAST = 160
 VECTOR_COLS = 336
 DMA_ALIGN = 256
 
@@ -71,18 +71,28 @@ def tile_rows_glin_sigmoid_bias_res_kernel(tc, x, w_words, w_scales, b, r, out):
         nc.vector.memset(w_plane[:].bitcast(I32), 0)
         nc.vector.memset(warm[:], 0.0)
 
-        def load_scales(g):
-            nc.scalar.dma_start(out=w_plane[ROWS * g : ROWS * g + 4, :].bitcast(I32), in_=w_scales[g].bitcast(I32))
+        def load_scales(queue, g):
+            queue.dma_start(out=w_plane[ROWS * g : ROWS * g + 4, :].bitcast(I32), in_=w_scales[g].bitcast(I32))
 
-        nc.scalar.dma_start(out=words[:].bitcast(I32), in_=w_words.rearrange("g p c -> (g p) c").bitcast(I32))
+        def load_words(queue):
+            queue.dma_start(out=words[:].bitcast(I32), in_=w_words.rearrange("g p c -> (g p) c").bitcast(I32))
+
+        def load_bias(queue):
+            queue.dma_start(out=b_rows[0:P:32, :, :], in_=b.rearrange("g (q j) o -> q g (j o)", j=32))
+
+        def load_r(i):
+            nc.sync.dma_start(out=r_tiles[i][:], in_=in_hbm(r, r_blocks[i]))
+
         nc.sync.dma_start(out=raw[0][:], in_=x_rows[:, :, 0:FIRST])
-        nc.scalar.dma_start(out=b_rows[0:P:32, :, :], in_=b.rearrange("g (q j) o -> q g (j o)", j=32))
-        for g in range(G):
-            load_scales(g)
-        nc.scalar.activation(out=warm[:], in_=warm[:], func=SIGMOID)
+        load_words(nc.sync)
+        load_scales(nc.sync, 0)
+        load_bias(nc.sync)
         nc.sync.dma_start(out=raw[1][:], in_=x_rows[:, :, FIRST:N])
-        for i, block in enumerate(r_blocks):
-            nc.sync.dma_start(out=r_tiles[i][:], in_=in_hbm(r, block))
+        nc.scalar.activation(out=warm[:], in_=warm[:], func=SIGMOID)
+        for g in range(1, G):
+            load_scales(nc.sync, g)
+        for i in range(len(r_blocks)):
+            load_r(i)
 
         def interleave(copy, c0, c1):
             src, base = (raw[0], 0) if c0 < FIRST else (raw[1], FIRST)
@@ -132,6 +142,7 @@ def tile_rows_glin_sigmoid_bias_res_kernel(tc, x, w_words, w_scales, b, r, out):
 
         for i, block in enumerate(out_blocks):
             for h, g in units(block):
-                nc.scalar.activation(out=y[h, g], in_=acc[h, g][:], func=SIGMOID, bias=bias[:, g, 0:1])
-                nc.vector.tensor_add(out=y[h, g], in0=y[h, g], in1=res[h, g])
+                for cols in (slice(0, QUARTER), slice(QUARTER, HALF)):
+                    nc.scalar.activation(out=y[h, g][:, cols], in_=acc[h, g][:, cols], func=SIGMOID, bias=bias[:, g, 0:1])
+                    nc.vector.tensor_add(out=y[h, g][:, cols], in0=y[h, g][:, cols], in1=res[h, g][:, cols])
             nc.sync.dma_start(out=in_hbm(out, block), in_=y_tiles[i][:])

@@ -19,9 +19,9 @@ PACK = 4
 ROWS = D // PACK
 HALF = 512
 QUARTER = HALF // 2
-FIRST = 576
-SCALAR_LAST = 160
-VECTOR_COLS = 336
+FIRST = 640
+SCALAR_LAST = 128
+VECTOR_COLS = 352
 DMA_ALIGN = 256
 
 
@@ -56,8 +56,8 @@ def tile_rows_glin_sigmoid_bias_res_kernel(tc, x, w_words, w_scales, b, r, out):
 
         words = pool.tile([P, 2 * M], U8, align_bytes=256)
         w_plane = pool.tile([P, M], U8, align_bytes=64)
-        b_rows = pool.tile([P, G, 32], F32, align_bytes=64)
-        bias = pool.tile([P, G, 32], F32, align_bytes=64)
+        b_rows = pool.tile([P, 32], F32, align_bytes=64)
+        bias = pool.tile([P, 32], F32, align_bytes=64)
         warm = pool.tile([P, 1], F32)
         raw = [pool.tile([P, PACK, w], F32, name="raw%d" % i, align_bytes=DMA_ALIGN) for i, w in enumerate((FIRST, N - FIRST))]
         grouped = pool.tile([P, N, PACK], BF16, align_bytes=64)
@@ -78,7 +78,7 @@ def tile_rows_glin_sigmoid_bias_res_kernel(tc, x, w_words, w_scales, b, r, out):
             queue.dma_start(out=words[:].bitcast(I32), in_=w_words.rearrange("g p c -> (g p) c").bitcast(I32))
 
         def load_bias(queue):
-            queue.dma_start(out=b_rows[0:P:32, :, :], in_=b.rearrange("g (q j) o -> q g (j o)", j=32))
+            queue.dma_start(out=b_rows[0:P:8, :], in_=b.rearrange("g (q j) o -> q g (j o)", j=32))
 
         def load_r(i):
             nc.sync.dma_start(out=r_tiles[i][:], in_=in_hbm(r, r_blocks[i]))
@@ -127,7 +127,7 @@ def tile_rows_glin_sigmoid_bias_res_kernel(tc, x, w_words, w_scales, b, r, out):
         interleave(nc.vector.tensor_copy, QUARTER, VECTOR_COLS)
         quantize(0, QUARTER)
         quantize(QUARTER, HALF)
-        nc.vector.transpose(out=bias[:].rearrange("p g j -> p (g j)"), in_=b_rows[:].rearrange("p g j -> p (g j)"))
+        nc.vector.transpose(out=bias[:], in_=b_rows[:])
         for h, g in order:
             if h == 0:
                 multiply(h, g)
@@ -143,6 +143,6 @@ def tile_rows_glin_sigmoid_bias_res_kernel(tc, x, w_words, w_scales, b, r, out):
         for i, block in enumerate(out_blocks):
             for h, g in units(block):
                 for cols in (slice(0, QUARTER), slice(QUARTER, HALF)):
-                    nc.scalar.activation(out=y[h, g][:, cols], in_=acc[h, g][:, cols], func=SIGMOID, bias=bias[:, g, 0:1])
+                    nc.scalar.activation(out=y[h, g][:, cols], in_=acc[h, g][:, cols], func=SIGMOID, bias=bias[:, 8 * g : 8 * g + 1])
                     nc.vector.tensor_add(out=y[h, g][:, cols], in0=y[h, g][:, cols], in1=res[h, g][:, cols])
             nc.sync.dma_start(out=in_hbm(out, block), in_=y_tiles[i][:])

@@ -28,8 +28,8 @@ DMA_ALIGN = 256
 def tile_rows_glin_sigmoid_bias_res_kernel(tc, x, w_words, w_scales, b, r, out):
     nc = tc.nc
     halves = [slice(h * HALF, (h + 1) * HALF) for h in range(N // HALF)]
-    r_blocks = [(0, 2, 0, 1), (2, 4, 0, 1), (0, 2, 1, 2), (2, 4, 1, 2)]
-    out_blocks = [(0, 2, 0, 1), (2, 4, 0, 1), (0, 2, 1, 2), (2, 4, 1, 2)]
+    r_blocks = [(0, 2, 0, 1), (2, 3, 0, 2), (3, 4, 0, 2), (0, 2, 1, 2)]
+    out_blocks = [(0, 2, 0, 1), (2, 3, 0, 2), (3, 4, 0, 2), (0, 2, 1, 2)]
     x_rows = x.rearrange("g (p j) n -> (g p) j n", j=PACK)
 
     def units(block):
@@ -128,16 +128,16 @@ def tile_rows_glin_sigmoid_bias_res_kernel(tc, x, w_words, w_scales, b, r, out):
         quantize(0, QUARTER)
         quantize(QUARTER, HALF)
         nc.vector.transpose(out=bias[:], in_=b_rows[:])
-        for h, g in order:
-            if h == 0:
-                multiply(h, g)
+        early = [u for u in order if u[0] == 0][:3]
+        for h, g in early:
+            multiply(h, g)
         interleave(nc.scalar.copy, N - SCALAR_LAST, N)
         interleave(nc.vector.tensor_copy, FIRST, HALF + QUARTER)
         interleave(nc.vector.tensor_copy, HALF + QUARTER, N - SCALAR_LAST)
         quantize(HALF, HALF + QUARTER)
         quantize(HALF + QUARTER, N)
         for h, g in order:
-            if h == 1:
+            if (h, g) not in early:
                 multiply(h, g)
 
         for i, block in enumerate(out_blocks):

from contextlib import ExitStack

import concourse.mybir as mybir

G, D, M, N = 4, 128, 128, 1024
FLOPS = 2 * G * D * M * N

F32 = mybir.dt.float32
BF16 = mybir.dt.bfloat16
I32 = mybir.dt.int32
U32 = mybir.dt.uint32
U8 = mybir.dt.uint8
FP8X4 = mybir.dt.float8_e4m3fn_x4
FP4X4 = mybir.dt.float4_e2m1fn_x4
SIGMOID = mybir.ActivationFunctionType.Sigmoid

P = 128
PACK = 4
ROWS = D // PACK
HALF = 512
QUARTER = HALF // 2
FIRST = 640
SCALAR_LAST = 128
VECTOR_COLS = 352
DMA_ALIGN = 256


def tile_rows_glin_sigmoid_bias_res_kernel(tc, x, w_words, w_scales, b, r, out):
    nc = tc.nc
    halves = [slice(h * HALF, (h + 1) * HALF) for h in range(N // HALF)]
    r_blocks = [(0, 2, 0, 1), (2, 3, 0, 2), (3, 4, 0, 2), (0, 2, 1, 2)]
    out_blocks = [(0, 2, 0, 1), (2, 3, 0, 2), (3, 4, 0, 2), (0, 2, 1, 2)]
    x_rows = x.rearrange("g (p j) n -> (g p) j n", j=PACK)

    def units(block):
        g0, g1, h0, h1 = block
        return [(h, g) for g in range(g0, g1) for h in range(h0, h1)]

    def in_hbm(t, block):
        g0, g1, h0, h1 = block
        return t[g0:g1, :, h0 * HALF : h1 * HALF].rearrange("g m n -> m g n")

    with ExitStack() as ctx:
        pool = ctx.enter_context(tc.tile_pool(name="sbuf", bufs=1))
        psum = ctx.enter_context(tc.psum_pool(name="psum", bufs=1))
        ctx.enter_context(tc.manual_schedule())

        def block_tiles(name, blocks):
            tiles, views = [], {}
            for i, (g0, g1, h0, h1) in enumerate(blocks):
                t = pool.tile([P, g1 - g0, (h1 - h0) * HALF], F32, name="%s%d" % (name, i), align_bytes=DMA_ALIGN)
                tiles.append(t)
                for h, g in units((g0, g1, h0, h1)):
                    views[h, g] = t[:, g - g0, (h - h0) * HALF : (h - h0 + 1) * HALF]
            return tiles, views

        words = pool.tile([P, 2 * M], U8, align_bytes=256)
        w_plane = pool.tile([P, M], U8, align_bytes=64)
        b_rows = pool.tile([P, 32], F32, align_bytes=64)
        bias = pool.tile([P, 32], F32, align_bytes=64)
        warm = pool.tile([P, 1], F32)
        raw = [pool.tile([P, PACK, w], F32, name="raw%d" % i, align_bytes=DMA_ALIGN) for i, w in enumerate((FIRST, N - FIRST))]
        grouped = pool.tile([P, N, PACK], BF16, align_bytes=64)
        codes = pool.tile([P, N], U32, align_bytes=64)
        x_plane = pool.tile([P, N], U8, align_bytes=64)
        r_tiles, res = block_tiles("res", r_blocks)
        y_tiles, y = block_tiles("y", out_blocks)
        acc = {(h, g): psum.tile([M, HALF], F32, name="acc%d_%d" % (h, g)) for h in range(2) for g in range(G)}

        nc.vector.memset(b_rows[:], 0.0)
        nc.vector.memset(w_plane[:].bitcast(I32), 0)
        nc.vector.memset(warm[:], 0.0)

        def load_scales(queue, g):
            queue.dma_start(out=w_plane[ROWS * g : ROWS * g + 4, :].bitcast(I32), in_=w_scales[g].bitcast(I32))

        def load_words(queue):
            queue.dma_start(out=words[:].bitcast(I32), in_=w_words.rearrange("g p c -> (g p) c").bitcast(I32))

        def load_bias(queue):
            queue.dma_start(out=b_rows[0:P:8, :], in_=b.rearrange("g (q j) o -> q g (j o)", j=32))

        def load_r(i):
            nc.sync.dma_start(out=r_tiles[i][:], in_=in_hbm(r, r_blocks[i]))

        nc.sync.dma_start(out=raw[0][:], in_=x_rows[:, :, 0:FIRST])
        load_words(nc.sync)
        load_scales(nc.sync, 0)
        load_bias(nc.sync)
        nc.sync.dma_start(out=raw[1][:], in_=x_rows[:, :, FIRST:N])
        nc.scalar.activation(out=warm[:], in_=warm[:], func=SIGMOID)
        for g in range(1, G):
            load_scales(nc.sync, g)
        for i in range(len(r_blocks)):
            load_r(i)

        def interleave(copy, c0, c1):
            src, base = (raw[0], 0) if c0 < FIRST else (raw[1], FIRST)
            copy(
                out=grouped[:, c0:c1, :].rearrange("p (c i) t -> p c t i", i=4),
                in_=src[:, :, c0 - base : c1 - base].rearrange("p t (c i) -> p c t i", i=4),
            )

        def quantize(c0, c1):
            nc.vector.quantize_mx(
                out=codes[:, c0:c1].bitcast(FP8X4),
                scales=x_plane[:, c0:c1],
                in_=grouped[:, c0:c1, :].rearrange("p c t -> p (c t)"),
            )

        def multiply(h, g):
            rows = slice(ROWS * g, ROWS * (g + 1))
            nc.tensor.matmul_mx(
                out=acc[h, g][:],
                lhsT=words[rows, :].bitcast(FP4X4),
                lhsT_scale=w_plane[rows, :],
                rhs=codes[rows, halves[h]].bitcast(FP8X4),
                rhs_scale=x_plane[rows, halves[h]],
                start=True,
                stop=True,
            )

        order = [u for block in out_blocks for u in units(block)]
        interleave(nc.scalar.copy, VECTOR_COLS, HALF)
        interleave(nc.scalar.copy, HALF, FIRST)
        interleave(nc.vector.tensor_copy, 0, QUARTER)
        interleave(nc.vector.tensor_copy, QUARTER, VECTOR_COLS)
        quantize(0, QUARTER)
        quantize(QUARTER, HALF)
        nc.vector.transpose(out=bias[:], in_=b_rows[:])
        early = [u for u in order if u[0] == 0][:3]
        for h, g in early:
            multiply(h, g)
        interleave(nc.scalar.copy, N - SCALAR_LAST, N)
        interleave(nc.vector.tensor_copy, FIRST, HALF + QUARTER)
        interleave(nc.vector.tensor_copy, HALF + QUARTER, N - SCALAR_LAST)
        quantize(HALF, HALF + QUARTER)
        quantize(HALF + QUARTER, N)
        for h, g in order:
            if (h, g) not in early:
                multiply(h, g)

        for i, block in enumerate(out_blocks):
            for h, g in units(block):
                for cols in (slice(0, QUARTER), slice(QUARTER, HALF)):
                    nc.scalar.activation(out=y[h, g][:, cols], in_=acc[h, g][:, cols], func=SIGMOID, bias=bias[:, 8 * g : 8 * g + 1])
                    nc.vector.tensor_add(out=y[h, g][:, cols], in0=y[h, g][:, cols], in1=res[h, g][:, cols])
            nc.sync.dma_start(out=in_hbm(out, block), in_=y_tiles[i][:])
